import numpy as np
import ml_dtypes


def mxq(x, axis, fmt="e4m3"):
    dtype, down = {"e4m3": (ml_dtypes.float8_e4m3fn, 7), "e5m2": (ml_dtypes.float8_e5m2, 14)}[fmt]
    v = np.moveaxis(np.asarray(x, np.float32).astype(ml_dtypes.bfloat16).astype(np.float64), axis, -1)
    blocks = v.reshape(v.shape[:-1] + (-1, 32))
    amax = np.abs(blocks).max(-1, keepdims=True)
    byte = np.maximum(np.where(amax > 0, np.frexp(amax)[1] - 1 + 127, 0) - down, 1)
    scale = np.exp2(byte - 127.0)
    codes = (blocks / scale).astype(np.float32).astype(dtype).astype(np.float64)
    return np.moveaxis((codes * scale).reshape(v.shape), -1, axis)


WIDE = False


def mx_kscale(k, group=512):
    if not WIDE:
        return np.ones(k)
    levels = np.array([10, -10, 5, -5, 0])
    if group != 512:
        return np.exp2(np.random.permutation(np.resize(levels, k // group))).repeat(group)
    if k % 512:
        return np.exp2(np.random.permutation(np.resize(levels, k // 32))).repeat(32)
    a = np.empty((k // 512, 16))
    for p in range(k // 512):
        a[p, :8] = np.random.permutation(np.resize(levels, 8))
        for g in range(8):
            far = levels[np.abs(levels - a[p, g]) >= 10]
            a[p, g + 8] = far[np.random.randint(len(far))]
    return np.exp2(a.ravel()).repeat(32)


def f64(x):
    return np.asarray(x).astype(np.float64)


def striped(idx):
    return np.tile(np.asarray(idx).reshape(-1, 16).T, (8, 1)).astype(np.uint16)


def unstriped(offs):
    return offs[:16].T.reshape(-1).astype(np.int64)


H, KV, D, NQ, N = 2, 2, 256, 512, 1024
CAP = 2.0


def setup_inputs():
    n = np.random.standard_normal
    s = mx_kscale(D, 0)[:, None]
    u = mx_kscale(N)
    t = np.random.uniform(0.5, 2.0, N) * u
    v = n((KV, N, 128))
    v[:, :, 127] = 1.0
    return {
        "qT": (n((H, D, NQ)) * s * (0.70 / np.sqrt(D))).astype(np.float32),
        "kT": (n((KV, D, N)) / s).astype(np.float32),
        "t": t.reshape(N, 1).astype(np.float32),
        "v": (v / t[:, None]).astype(np.float32),
        "kb": (0.5 * n((N, 1))).astype(np.float32),
        "sink": (N * np.random.uniform(0.1, 1.0, (H, NQ, 1))).astype(np.float32),
    }


def reference(qT, kT, t, v, kb, sink):
    a = mxq(f64(kT), 1, "e4m3").transpose(0, 2, 1) @ mxq(f64(qT), 1, "e4m3")
    a = a + f64(kb)
    a = CAP * np.tanh(a / CAP)
    p = np.exp(a)
    w = p * f64(t)
    y = mxq(w, 1, "e4m3").transpose(0, 2, 1) @ mxq(f64(v), 1, "e4m3")
    y = y / (y[:, :, 127:128] + f64(sink))
    return y

@@ -1,0 +1,283 @@
+from contextlib import ExitStack
+
+import concourse.mybir as mybir
+
+H, D, NQ, N, E = 2, 256, 512, 1024, 128
+CAP = 2.0
+FLOPS = 2 * H * NQ * N * (D + E)
+
+F32 = mybir.dt.float32
+BF16 = mybir.dt.bfloat16
+U32 = mybir.dt.uint32
+U8 = mybir.dt.uint8
+FP8X4 = mybir.dt.float8_e4m3fn_x4
+ACT = mybir.ActivationFunctionType
+ALU = mybir.AluOpType
+
+P = 128
+PACK = 4
+ROWS = D // PACK
+PASS = P * PACK
+PASSES = N // PASS
+QT = 128
+SCORE_BANKS = 3
+
+
+def tile_rows_a_exp_kb_cap_sink_kernel(tc, qT, kT, t, v, kb, sink, out):
+    nc = tc.nc
+    with ExitStack() as ctx:
+        sb = ctx.enter_context(tc.tile_pool(name="sb", bufs=1))
+        ps = ctx.enter_context(tc.psum_pool(name="ps", bufs=1))
+        ctx.enter_context(tc.manual_schedule())
+
+        def tile(name, shape, dtype):
+            return sb.tile(shape, dtype, name=name, tag=name, align_bytes=64)
+
+        q_hbm = qT.rearrange("h (p j) n -> (h p) j n", j=PACK)
+        k_hbm = kT.rearrange("h (p j) n -> (h p) j n", j=PACK)
+
+        def load(name, src, queue):
+            raw = tile(name, list(src.shape), F32)
+            queue.dma_start(out=raw[:], in_=src)
+            return raw
+
+        half = PASS // 2
+        k0a = load("k0a", k_hbm[:, :, 0:half], nc.sync)
+        k0b = load("k0b", k_hbm[:, :, half:PASS], nc.sync)
+        q0 = load("q0", q_hbm[:, :, 0:QT], nc.sync)
+        kb_sb = load("kb", kb.rearrange("(c p r) o -> p c (r o)", p=P, r=PACK), nc.scalar)
+        t_sb = load("t", t.rearrange("(c p r) o -> p c (r o)", p=P, r=PACK), nc.scalar)
+        q1 = load("q1", q_hbm[:, :, QT:NQ], nc.sync)
+        k1 = load("k1", k_hbm[:, :, PASS:N], nc.sync)
+        v_raw = load("v", v.rearrange("h (c p r) e -> p (h c) (r e)", p=P, r=PACK), nc.sync)
+        sink_sb = tile("sink", [P, H * NQ // QT], F32)
+        with nc.allow_non_contiguous_dma(reason="one sink value a partition and query tile"):
+            nc.sync.dma_start(out=sink_sb[:], in_=sink.rearrange("h (a p) o -> p (h a o)", p=P))
+
+        def quantize(codes, scales, src, a, b):
+            nc.vector.quantize_mx(out=codes[:, a:b].bitcast(FP8X4), scales=scales[:, a:b],
+                                  in_=src[:, PACK * a:PACK * b])
+
+        k16 = [tile("k16_%d" % c, [P, PASS * PACK], BF16) for c in range(PASSES)]
+        k_codes = [tile("kc%d" % c, [P, PASS], U32) for c in range(PASSES)]
+        k_scales = [tile("ks%d" % c, [P, PASS], U8) for c in range(PASSES)]
+        q16 = [tile("q16_0", [P, QT * PACK], BF16), tile("q16_1", [P, (NQ - QT) * PACK], BF16)]
+        q_codes = [tile("qc0", [P, QT], U32), tile("qc1", [P, NQ - QT], U32)]
+        q_scales = [tile("qs0", [P, QT], U8), tile("qs1", [P, NQ - QT], U8)]
+        v16 = tile("v16", [P, H * PASSES * E * PACK], BF16)
+        v_codes = tile("vc", [P, H * PASSES * E], U32)
+        v_scales = tile("vs", [P, H * PASSES * E], U8)
+        kb_half = tile("kbh", [P, PASSES, PACK], F32)
+
+        def round_keys(c, raw, s0):
+            n = raw.shape[2] // PACK
+            dst = k16[c][:].rearrange("p (r s j) -> p s j r", r=PACK, j=PACK)
+            nc.vector.tensor_copy(out=dst[:, s0:s0 + n], in_=raw[:].rearrange("p j (s r) -> p s j r", r=PACK))
+
+        def round_queries(x, raw):
+            nc.vector.tensor_copy(out=q16[x][:].rearrange("p (a i j) -> p a j i", i=2, j=PACK),
+                                  in_=raw[:].rearrange("p j (a i) -> p a j i", i=2))
+
+        def round_values():
+            nc.vector.tensor_copy(out=v16[:].rearrange("p (x a i r) -> p x a r i", x=H * PASSES, i=2, r=PACK),
+                                  in_=v_raw[:].rearrange("p x (r a i) -> p x a r i", r=PACK, i=2))
+
+        def q_operand(g, qt):
+            x = min(qt, 1)
+            cols = slice((qt - x) * QT, (qt - x + 1) * QT)
+            rows = slice(ROWS * g, ROWS * (g + 1))
+            return q_codes[x][rows, cols], q_scales[x][rows, cols]
+
+        groups = [(0, 0, 0, 1), (0, 1, 0, 1), (0, 0, 1, 3), (0, 1, 1, 3), (1, 0, 0, 4), (1, 1, 0, 3), (1, 1, 3, 1)]
+        capped = [tile("th%d" % i, [P, PACK, n * QT], F32) for i, (c, g, a, n) in enumerate(groups)]
+        units = [(i, r) for r in range(PACK) for i in (0, 1)]
+        units.extend([(i, r) for i in range(2, len(groups)) for r in range(PACK)])
+        banks = {}
+        pending = list(units)
+        issued = [0, 0]
+        freed = [0, 0]
+        ready = set()
+
+        def issue_scores():
+            while pending and pending[0][0] in ready:
+                i, r = pending[0]
+                c, g, a, n = groups[i]
+                if issued[g] - freed[g] == SCORE_BANKS:
+                    return
+                pending.remove((i, r))
+                tag = "s%d_%d" % (g, issued[g] % SCORE_BANKS)
+                issued[g] = issued[g] + 1
+                bank = ps.tile([P, 512], F32, name=tag, tag=tag)
+                rows = slice(ROWS * g, ROWS * (g + 1))
+                cols = slice(r * P, (r + 1) * P)
+                for x in range(n):
+                    qc, qs = q_operand(g, a + x)
+                    nc.tensor.matmul_mx(out=bank[:, x * QT:(x + 1) * QT], lhsT=k_codes[c][rows, cols].bitcast(FP8X4),
+                                        lhsT_scale=k_scales[c][rows, cols], rhs=qc.bitcast(FP8X4), rhs_scale=qs,
+                                        start=True, stop=True)
+                banks[(i, r)] = bank
+
+        def cap(i, r):
+            c, g, a, n = groups[i]
+            nc.scalar.activation(out=capped[i][:, r, :], in_=banks[(i, r)][:, 0:n * QT], func=ACT.Tanh,
+                                 bias=kb_half[:, c, r:r + 1], scale=1.0 / CAP)
+            freed[g] = freed[g] + 1
+            issue_scores()
+
+        probs = {}
+        w16 = [tile("w16_%d" % i, [P, n * QT * PACK], BF16) for i, (c, g, a, n) in enumerate(groups)]
+        w_codes = [tile("wc%d" % i, [P, n * QT], U32) for i, (c, g, a, n) in enumerate(groups)]
+        w_scales = [tile("ws%d" % i, [P, n * QT], U8) for i, (c, g, a, n) in enumerate(groups)]
+
+        def exp(i, a, b):
+            p = tile("p%d_%d" % (i, a), [P, PACK, b - a], F32)
+            nc.scalar.activation(out=p[:], in_=capped[i][:, :, a:b], func=ACT.Exp, scale=CAP)
+            probs[(i, a)] = p
+
+        def weigh(i, a, b, a0=None):
+            a0 = a if a0 is None else a0
+            c = groups[i][0]
+            n = (b - a) // 2
+            nc.vector.tensor_tensor(
+                out=w16[i][:, PACK * a:PACK * b].rearrange("p (a i r) -> p a r i", i=2, r=PACK),
+                in0=probs[(i, a0)][:, :, a - a0:b - a0].rearrange("p r (a i) -> p a r i", i=2),
+                in1=t_sb[:, c, :].unsqueeze(1).unsqueeze(3).to_broadcast([P, n, PACK, 2]),
+                op=ALU.mult)
+
+        def quantize_w(i, a, b):
+            quantize(w_codes[i], w_scales[i], w16[i], a, b)
+
+        def w_operand(c, g, qt):
+            i = [x for x, (cc, gg, a, n) in enumerate(groups) if cc == c and gg == g and a <= qt < a + n][0]
+            cols = slice((qt - groups[i][2]) * QT, (qt - groups[i][2] + 1) * QT)
+            return w_codes[i][:, cols], w_scales[i][:, cols]
+
+        def values_pass(y, x, g, qt, c):
+            wc, ws = w_operand(c, g, qt)
+            cols = slice((g * PASSES + c) * E, (g * PASSES + c + 1) * E)
+            nc.tensor.matmul_mx(out=y[:, x, :], lhsT=wc.bitcast(FP8X4), lhsT_scale=ws,
+                                rhs=v_codes[:, cols].bitcast(FP8X4), rhs_scale=v_scales[:, cols],
+                                start=(c == 0), stop=(c == PASSES - 1))
+
+        def values(y, x, g, qt):
+            for c in range(PASSES):
+                values_pass(y, x, g, qt, c)
+
+        def denominators(y, g, a, n):
+            den = tile("den%d_%d" % (g, a), [P, n], F32)
+            col = g * (NQ // QT) + a
+            nc.vector.tensor_tensor(out=den[:], in0=y[:, 0:n, E - 1], in1=sink_sb[:, col:col + n], op=ALU.add)
+            return den
+
+        def invert(den, g, a, n):
+            inv = tile("inv%d_%d" % (g, a), [P, n], F32)
+            nc.vector.reciprocal(out=inv[:], in_=den[:])
+            return inv
+
+        def store(res, g, a, n):
+            nc.sync.dma_start(out=out[g, a * QT:(a + n) * QT, :].rearrange("(x p) e -> p x e", p=P), in_=res[:])
+
+        round_keys(0, k0a, 0)
+        nc.vector.tensor_scalar(out=kb_half[:], in0=kb_sb[:], scalar1=1.0 / CAP, scalar2=None, op0=ALU.mult)
+        round_keys(0, k0b, half // PACK)
+        round_queries(0, q0)
+        quantize(k_codes[0], k_scales[0], k16[0], 0, P)
+        quantize(q_codes[0], q_scales[0], q16[0], 0, QT)
+        quantize(k_codes[0], k_scales[0], k16[0], P, 2 * P)
+        quantize(k_codes[0], k_scales[0], k16[0], 2 * P, 4 * P)
+        ready.add(0)
+        ready.add(1)
+        issue_scores()
+        round_queries(1, q1)
+        quantize(q_codes[1], q_scales[1], q16[1], 0, QT)
+        quantize(q_codes[1], q_scales[1], q16[1], QT, 3 * QT)
+        ready.add(2)
+        ready.add(3)
+        for r in range(PACK):
+            cap(0, r)
+            cap(1, r)
+        exp(0, 0, QT)
+        exp(1, 0, QT)
+        weigh(0, 0, QT)
+        weigh(1, 0, QT)
+        quantize_w(0, 0, QT)
+        round_keys(1, k1, 0)
+        quantize_w(1, 0, QT)
+        quantize(k_codes[1], k_scales[1], k16[1], 0, PASS)
+        for i in (4, 5, 6):
+            ready.add(i)
+        for r in range(PACK):
+            cap(2, r)
+        round_values()
+        cap(3, 0)
+        exp(2, 0, 3 * QT)
+        quantize(v_codes, v_scales, v16, 0, H * PASSES * E)
+        weigh(2, 0, 3 * QT)
+        quantize_w(2, 0, QT)
+        quantize_w(2, QT, 3 * QT)
+        for r in range(1, PACK):
+            cap(3, r)
+        cap(4, 0)
+        exp(3, 0, 3 * QT)
+        weigh(3, 0, 3 * QT)
+        quantize_w(3, 0, QT)
+        quantize_w(3, QT, 3 * QT)
+        for r in range(1, PACK):
+            cap(4, r)
+        cap(5, 0)
+        exp(4, 0, 2 * QT)
+        weigh(4, 0, 2 * QT)
+        cap(5, 1)
+        cap(5, 2)
+        exp(4, 2 * QT, 4 * QT)
+        quantize_w(4, 0, 2 * QT)
+        weigh(4, 2 * QT, 4 * QT)
+        cap(5, 3)
+        y0 = ps.tile([P, 4, E], F32, name="y0", tag="y0")
+        values(y0, 0, 0, 0)
+        values(y0, 1, 0, 1)
+        cap(6, 0)
+        exp(5, 0, QT)
+        quantize_w(4, 2 * QT, 4 * QT)
+        weigh(5, 0, QT)
+        values(y0, 2, 0, 2)
+        values(y0, 3, 0, 3)
+        cap(6, 1)
+        exp(5, QT, 2 * QT)
+        den0 = denominators(y0, 0, 0, 4)
+        quantize_w(5, 0, QT)
+        inv0 = invert(den0, 0, 0, 4)
+        weigh(5, QT, 2 * QT)
+        y1 = ps.tile([P, 4, E], F32, name="y1", tag="y1")
+        values(y1, 0, 1, 0)
+        res0 = tile("res0", [P, 4, E], F32)
+        nc.vector.tensor_tensor(out=res0[:], in0=y0[:], in1=inv0[:].unsqueeze(2).to_broadcast([P, 4, E]), op=ALU.mult)
+        store(res0, 0, 0, 4)
+        quantize_w(5, QT, 2 * QT)
+        values(y1, 1, 1, 1)
+        cap(6, 2)
+        cap(6, 3)
+        exp(5, 2 * QT, 3 * QT)
+        exp(6, 0, QT // 2)
+        exp(6, QT // 2, QT)
+        y2 = ps.tile([P, 4, E], F32, name="y2", tag="y0")
+        values_pass(y2, 0, 1, 3, 0)
+        weigh(5, 2 * QT, 3 * QT)
+        weigh(6, 0, QT // 2)
+        quantize_w(5, 2 * QT, 3 * QT)
+        values(y1, 2, 1, 2)
+        weigh(6, QT // 2, QT)
+        quantize_w(6, 0, QT // 2)
+        quantize_w(6, QT // 2, QT)
+        values_pass(y2, 0, 1, 3, 1)
+        den1 = denominators(y1, 1, 0, 3)
+        inv1 = invert(den1, 1, 0, 3)
+        den2 = denominators(y2, 1, 3, 1)
+        inv2 = invert(den2, 1, 3, 1)
+        res1 = tile("res1", [P, 3, E], F32)
+        for x in range(3):
+            nc.scalar.activation(out=res1[:, x, :], in_=y1[:, x, :], func=ACT.Copy, scale=inv1[:, x:x + 1])
+        store(res1, 1, 0, 3)
+        res2 = tile("res2", [P, 1, E], F32)
+        nc.vector.tensor_scalar(out=res2[:, 0, :], in0=y2[:, 0, :], scalar1=inv2[:, 0:1], scalar2=None, op0=ALU.mult)
+        store(res2, 1, 3, 1)

@@ -21,6 +21,7 @@ PASS = P * PACK
 PASSES = N // PASS
 QT = 128
 SCORE_BANKS = 3
+RUN = 4
 
 
 def tile_rows_a_exp_kb_cap_sink_kernel(tc, qT, kT, t, v, kb, sink, out):
@@ -45,8 +46,8 @@ def tile_rows_a_exp_kb_cap_sink_kernel(tc, qT, kT, t, v, kb, sink, out):
         k0a = load("k0a", k_hbm[:, :, 0:half], nc.sync)
         k0b = load("k0b", k_hbm[:, :, half:PASS], nc.sync)
         q0 = load("q0", q_hbm[:, :, 0:QT], nc.sync)
-        kb_sb = load("kb", kb.rearrange("(c p r) o -> p c (r o)", p=P, r=PACK), nc.scalar)
         t_sb = load("t", t.rearrange("(c p r) o -> p c (r o)", p=P, r=PACK), nc.scalar)
+        kb_sb = load("kb", kb.rearrange("(c p r) o -> p c (r o)", p=P, r=PACK), nc.scalar)
         q1 = load("q1", q_hbm[:, :, QT:NQ], nc.sync)
         k1 = load("k1", k_hbm[:, :, PASS:N], nc.sync)
         v_raw = load("v", v.rearrange("h (c p r) e -> p (h c) (r e)", p=P, r=PACK), nc.sync)
@@ -68,19 +69,28 @@ def tile_rows_a_exp_kb_cap_sink_kernel(tc, qT, kT, t, v, kb, sink, out):
         v_codes = tile("vc", [P, H * PASSES * E], U32)
         v_scales = tile("vs", [P, H * PASSES * E], U8)
         kb_half = tile("kbh", [P, PASSES, PACK], F32)
+        positive = tile("positive", [P, PASSES, PACK], F32)
+        sign_t = tile("sign_t", [P, PASSES, PACK], F32)
+        abs_t = tile("abs_t", [P, PASSES, PACK], F32)
+        log_t = tile("log_t", [P, PASSES, PACK], F32)
 
         def round_keys(c, raw, s0):
             n = raw.shape[2] // PACK
             dst = k16[c][:].rearrange("p (r s j) -> p s j r", r=PACK, j=PACK)
             nc.vector.tensor_copy(out=dst[:, s0:s0 + n], in_=raw[:].rearrange("p j (s r) -> p s j r", r=PACK))
 
-        def round_queries(x, raw):
-            nc.vector.tensor_copy(out=q16[x][:].rearrange("p (a i j) -> p a j i", i=2, j=PACK),
-                                  in_=raw[:].rearrange("p j (a i) -> p a j i", i=2))
+        def round_queries(x, raw, a, b):
+            nc.vector.tensor_copy(out=q16[x][:, PACK * a:PACK * b].rearrange("p (a i j) -> p a j i", i=RUN, j=PACK),
+                                  in_=raw[:, :, a:b].rearrange("p j (a i) -> p a j i", i=RUN))
 
-        def round_values():
-            nc.vector.tensor_copy(out=v16[:].rearrange("p (x a i r) -> p x a r i", x=H * PASSES, i=2, r=PACK),
-                                  in_=v_raw[:].rearrange("p x (r a i) -> p x a r i", r=PACK, i=2))
+        def round_values(c):
+            for g in range(H):
+                x = g * PASSES + c
+                nc.vector.tensor_tensor(
+                    out=v16[:, x * PASS:(x + 1) * PASS].rearrange("p (a i r) -> p a r i", i=RUN, r=PACK),
+                    in0=v_raw[:, x, :].rearrange("p (r a i) -> p a r i", r=PACK, i=RUN),
+                    in1=sign_t[:, c, :].unsqueeze(1).unsqueeze(3).to_broadcast([P, E // RUN, PACK, RUN]),
+                    op=ALU.mult)
 
         def q_operand(g, qt):
             x = min(qt, 1)
@@ -88,12 +98,15 @@ def tile_rows_a_exp_kb_cap_sink_kernel(tc, qT, kT, t, v, kb, sink, out):
             rows = slice(ROWS * g, ROWS * (g + 1))
             return q_codes[x][rows, cols], q_scales[x][rows, cols]
 
-        groups = [(0, 0, 0, 1), (0, 1, 0, 1), (0, 0, 1, 3), (0, 1, 1, 3), (1, 0, 0, 4), (1, 1, 0, 3), (1, 1, 3, 1)]
-        capped = [tile("th%d" % i, [P, PACK, n * QT], F32) for i, (c, g, a, n) in enumerate(groups)]
-        units = [(i, r) for r in range(PACK) for i in (0, 1)]
-        units.extend([(i, r) for i in range(2, len(groups)) for r in range(PACK)])
+        groups = [(0, [(0, 0, 1), (1, 0, 1)]), (0, [(0, 1, 3)]), (1, [(0, 0, 4), (1, 0, 1)]), (0, [(1, 1, 3)]), (1, [(1, 1, 2)]), (1, [(1, 3, 1)])]
+        widths = [sum(n for (g, a, n) in parts) * QT for (c, parts) in groups]
+        capped = [tile("th%d" % i, [P, PACK, w], F32) for i, w in enumerate(widths)]
+        rounded = [tile("p%d" % i, [P, PACK, w], BF16) for i, w in enumerate(widths)]
+        w16 = [tile("w16_%d" % i, [P, w * PACK], BF16) for i, w in enumerate(widths)]
+        w_codes = [tile("wc%d" % i, [P, w], U32) for i, w in enumerate(widths)]
+        w_scales = [tile("ws%d" % i, [P, w], U8) for i, w in enumerate(widths)]
+        pending = [(i, r) for i in range(len(groups)) for r in range(PACK)]
         banks = {}
-        pending = list(units)
         issued = [0, 0]
         freed = [0, 0]
         ready = set()
@@ -101,55 +114,55 @@ def tile_rows_a_exp_kb_cap_sink_kernel(tc, qT, kT, t, v, kb, sink, out):
         def issue_scores():
             while pending and pending[0][0] in ready:
                 i, r = pending[0]
-                c, g, a, n = groups[i]
-                if issued[g] - freed[g] == SCORE_BANKS:
+                c, parts = groups[i]
+                if any(issued[g] - freed[g] == SCORE_BANKS for (g, a, n) in parts):
                     return
                 pending.remove((i, r))
-                tag = "s%d_%d" % (g, issued[g] % SCORE_BANKS)
-                issued[g] = issued[g] + 1
-                bank = ps.tile([P, 512], F32, name=tag, tag=tag)
-                rows = slice(ROWS * g, ROWS * (g + 1))
+                for (g, a, n) in parts:
+                    tag = "s%d_%d" % (g, issued[g] % SCORE_BANKS)
+                    issued[g] = issued[g] + 1
+                    banks[(i, r, g)] = ps.tile([P, 512], F32, name=tag, tag=tag)
                 cols = slice(r * P, (r + 1) * P)
-                for x in range(n):
-                    qc, qs = q_operand(g, a + x)
-                    nc.tensor.matmul_mx(out=bank[:, x * QT:(x + 1) * QT], lhsT=k_codes[c][rows, cols].bitcast(FP8X4),
-                                        lhsT_scale=k_scales[c][rows, cols], rhs=qc.bitcast(FP8X4), rhs_scale=qs,
-                                        start=True, stop=True)
-                banks[(i, r)] = bank
+                for x in range(4):
+                    for (g, a, n) in [part for part in parts if x < part[2]]:
+                        rows = slice(ROWS * g, ROWS * (g + 1))
+                        qc, qs = q_operand(g, a + x)
+                        nc.tensor.matmul_mx(out=banks[(i, r, g)][:, x * QT:(x + 1) * QT],
+                                            lhsT=k_codes[c][rows, cols].bitcast(FP8X4),
+                                            lhsT_scale=k_scales[c][rows, cols], rhs=qc.bitcast(FP8X4), rhs_scale=qs,
+                                            start=True, stop=True)
 
         def cap(i, r):
-            c, g, a, n = groups[i]
-            nc.scalar.activation(out=capped[i][:, r, :], in_=banks[(i, r)][:, 0:n * QT], func=ACT.Tanh,
-                                 bias=kb_half[:, c, r:r + 1], scale=1.0 / CAP)
-            freed[g] = freed[g] + 1
+            c, parts = groups[i]
+            first = 0
+            for (g, a, n) in parts:
+                nc.scalar.activation(out=capped[i][:, r, first:first + n * QT], in_=banks[(i, r, g)][:, 0:n * QT],
+                                     func=ACT.Tanh, bias=kb_half[:, c, r:r + 1], scale=1.0 / CAP)
+                freed[g] = freed[g] + 1
+                first = first + n * QT
             issue_scores()
 
-        probs = {}
-        w16 = [tile("w16_%d" % i, [P, n * QT * PACK], BF16) for i, (c, g, a, n) in enumerate(groups)]
-        w_codes = [tile("wc%d" % i, [P, n * QT], U32) for i, (c, g, a, n) in enumerate(groups)]
-        w_scales = [tile("ws%d" % i, [P, n * QT], U8) for i, (c, g, a, n) in enumerate(groups)]
+        def weigh(i, r, a=0, b=None):
+            b = widths[i] if b is None else b
+            nc.scalar.activation(out=rounded[i][:, r, a:b], in_=capped[i][:, r, a:b], func=ACT.Exp, scale=CAP,
+                                 bias=log_t[:, groups[i][0], r:r + 1])
 
-        def exp(i, a, b):
-            p = tile("p%d_%d" % (i, a), [P, PACK, b - a], F32)
-            nc.scalar.activation(out=p[:], in_=capped[i][:, :, a:b], func=ACT.Exp, scale=CAP)
-            probs[(i, a)] = p
-
-        def weigh(i, a, b, a0=None):
-            a0 = a if a0 is None else a0
-            c = groups[i][0]
-            n = (b - a) // 2
-            nc.vector.tensor_tensor(
-                out=w16[i][:, PACK * a:PACK * b].rearrange("p (a i r) -> p a r i", i=2, r=PACK),
-                in0=probs[(i, a0)][:, :, a - a0:b - a0].rearrange("p r (a i) -> p a r i", i=2),
-                in1=t_sb[:, c, :].unsqueeze(1).unsqueeze(3).to_broadcast([P, n, PACK, 2]),
-                op=ALU.mult)
+        def interleave(i, a, b):
+            nc.vector.tensor_copy(
+                out=w16[i][:, PACK * a:PACK * b].rearrange("p (a i r) -> p a r i", i=RUN, r=PACK),
+                in_=rounded[i][:, :, a:b].rearrange("p r (a i) -> p a r i", i=RUN))
 
         def quantize_w(i, a, b):
             quantize(w_codes[i], w_scales[i], w16[i], a, b)
 
+        w_place = {}
+        for i, (c, parts) in enumerate(groups):
+            tiles = [(g, a + x) for (g, a, n) in parts for x in range(n)]
+            for x, (g, qt) in enumerate(tiles):
+                w_place[(c, g, qt)] = (i, slice(x * QT, (x + 1) * QT))
+
         def w_operand(c, g, qt):
-            i = [x for x, (cc, gg, a, n) in enumerate(groups) if cc == c and gg == g and a <= qt < a + n][0]
-            cols = slice((qt - groups[i][2]) * QT, (qt - groups[i][2] + 1) * QT)
+            i, cols = w_place[(c, g, qt)]
             return w_codes[i][:, cols], w_scales[i][:, cols]
 
         def values_pass(y, x, g, qt, c):
@@ -177,107 +190,117 @@ def tile_rows_a_exp_kb_cap_sink_kernel(tc, qT, kT, t, v, kb, sink, out):
         def store(res, g, a, n):
             nc.sync.dma_start(out=out[g, a * QT:(a + n) * QT, :].rearrange("(x p) e -> p x e", p=P), in_=res[:])
 
+        nc.scalar.activation(out=abs_t[:], in_=t_sb[:], func=ACT.Abs)
+        nc.scalar.activation(out=kb_half[:], in_=kb_sb[:], func=ACT.Copy, scale=1.0 / CAP)
+        nc.scalar.activation(out=log_t[:], in_=abs_t[:], func=ACT.Ln)
         round_keys(0, k0a, 0)
-        nc.vector.tensor_scalar(out=kb_half[:], in0=kb_sb[:], scalar1=1.0 / CAP, scalar2=None, op0=ALU.mult)
         round_keys(0, k0b, half // PACK)
-        round_queries(0, q0)
+        round_queries(0, q0, 0, QT)
         quantize(k_codes[0], k_scales[0], k16[0], 0, P)
         quantize(q_codes[0], q_scales[0], q16[0], 0, QT)
         quantize(k_codes[0], k_scales[0], k16[0], P, 2 * P)
         quantize(k_codes[0], k_scales[0], k16[0], 2 * P, 4 * P)
         ready.add(0)
-        ready.add(1)
         issue_scores()
-        round_queries(1, q1)
+        nc.vector.tensor_scalar(out=positive[:], in0=t_sb[:], scalar1=0.0, scalar2=2.0, op0=ALU.is_ge, op1=ALU.mult)
+        round_queries(1, q1, 0, QT)
+        round_queries(1, q1, QT, 3 * QT)
         quantize(q_codes[1], q_scales[1], q16[1], 0, QT)
         quantize(q_codes[1], q_scales[1], q16[1], QT, 3 * QT)
-        ready.add(2)
-        ready.add(3)
-        for r in range(PACK):
-            cap(0, r)
-            cap(1, r)
-        exp(0, 0, QT)
-        exp(1, 0, QT)
-        weigh(0, 0, QT)
-        weigh(1, 0, QT)
-        quantize_w(0, 0, QT)
+        ready.add(1)
+
+        def scale_rows(y, inv, g, a, n):
+            res = tile("res%d_%d" % (g, a), [P, n, E], F32)
+            nc.vector.tensor_tensor(out=res[:], in0=y[:, 0:n, :], in1=inv[:].unsqueeze(2).to_broadcast([P, n, E]),
+                                    op=ALU.mult)
+            store(res, g, a, n)
+
+        def scale_rows_act(y, inv, g, a, n):
+            res = tile("res%d_%d" % (g, a), [P, n, E], F32)
+            for x in range(n):
+                nc.scalar.activation(out=res[:, x, :], in_=y[:, x, :], func=ACT.Copy, scale=inv[:, x:x + 1])
+            store(res, g, a, n)
+
+        def scalar_group(i):
+            for r in range(PACK):
+                cap(i, r)
+                if r > 0:
+                    weigh(i, r - 1)
+                elif i > 1:
+                    weigh(i - 1, PACK - 1)
+
+        scalar_group(0)
+        weigh(0, 3)
+        nc.vector.tensor_scalar(out=sign_t[:], in0=positive[:], scalar1=1.0, scalar2=None, op0=ALU.subtract)
         round_keys(1, k1, 0)
-        quantize_w(1, 0, QT)
-        quantize(k_codes[1], k_scales[1], k16[1], 0, PASS)
-        for i in (4, 5, 6):
+        quantize(k_codes[1], k_scales[1], k16[1], 0, 2 * P)
+        quantize(k_codes[1], k_scales[1], k16[1], 2 * P, 4 * P)
+        for i in (2, 3, 4, 5):
             ready.add(i)
-        for r in range(PACK):
-            cap(2, r)
-        round_values()
-        cap(3, 0)
-        exp(2, 0, 3 * QT)
+        scalar_group(1)
+        interleave(0, 0, 2 * QT)
+        round_values(0)
+        quantize_w(0, 0, 2 * QT)
+        scalar_group(2)
+        interleave(1, 0, 3 * QT)
+        round_values(1)
+        quantize_w(1, 0, QT)
+        quantize_w(1, QT, 3 * QT)
         quantize(v_codes, v_scales, v16, 0, H * PASSES * E)
-        weigh(2, 0, 3 * QT)
-        quantize_w(2, 0, QT)
-        quantize_w(2, QT, 3 * QT)
-        for r in range(1, PACK):
-            cap(3, r)
+        ys = [ps.tile([P, 4, E], F32, name="y%d" % x, tag="y%d" % x) for x in range(2)]
+        cap(3, 0)
+        weigh(2, 3)
+        interleave(2, 0, 2 * QT)
+        interleave(2, 2 * QT, 5 * QT)
+        quantize_w(2, 0, 2 * QT)
+        quantize_w(2, 2 * QT, 4 * QT)
+        quantize_w(2, 4 * QT, 5 * QT)
+        cap(3, 1)
+        weigh(3, 0)
+        cap(3, 2)
+        values(ys[0], 0, 0, 0)
+        values(ys[0], 1, 0, 1)
+        weigh(3, 1)
+        cap(3, 3)
+        values(ys[0], 2, 0, 2)
+        values(ys[0], 3, 0, 3)
+        weigh(3, 2)
         cap(4, 0)
-        exp(3, 0, 3 * QT)
-        weigh(3, 0, 3 * QT)
+        values(ys[1], 0, 1, 0)
+        weigh(3, 3)
+        den = denominators(ys[0], 0, 0, 4)
+        interleave(3, 0, QT)
+        inv = invert(den, 0, 0, 4)
+        interleave(3, QT, 3 * QT)
+        scale_rows(ys[0], inv, 0, 0, 4)
         quantize_w(3, 0, QT)
         quantize_w(3, QT, 3 * QT)
         for r in range(1, PACK):
             cap(4, r)
+            weigh(4, r - 1)
         cap(5, 0)
-        exp(4, 0, 2 * QT)
-        weigh(4, 0, 2 * QT)
+        weigh(4, 3)
         cap(5, 1)
         cap(5, 2)
-        exp(4, 2 * QT, 4 * QT)
-        quantize_w(4, 0, 2 * QT)
-        weigh(4, 2 * QT, 4 * QT)
+        weigh(5, 0)
         cap(5, 3)
-        y0 = ps.tile([P, 4, E], F32, name="y0", tag="y0")
-        values(y0, 0, 0, 0)
-        values(y0, 1, 0, 1)
-        cap(6, 0)
-        exp(5, 0, QT)
-        quantize_w(4, 2 * QT, 4 * QT)
-        weigh(5, 0, QT)
-        values(y0, 2, 0, 2)
-        values(y0, 3, 0, 3)
-        cap(6, 1)
-        exp(5, QT, 2 * QT)
-        den0 = denominators(y0, 0, 0, 4)
+        y_last = ps.tile([P, 4, E], F32, name="y_last", tag="y0")
+        values_pass(y_last, 0, 1, 3, 0)
+        interleave(4, 0, QT)
+        interleave(4, QT, 2 * QT)
+        quantize_w(4, 0, QT)
+        quantize_w(4, QT, 2 * QT)
+        for x in range(2):
+            values(ys[1], 1 + x, 1, 1 + x)
+        weigh(5, 1)
+        weigh(5, 2)
+        weigh(5, 3)
+        interleave(5, 0, QT)
         quantize_w(5, 0, QT)
-        inv0 = invert(den0, 0, 0, 4)
-        weigh(5, QT, 2 * QT)
-        y1 = ps.tile([P, 4, E], F32, name="y1", tag="y1")
-        values(y1, 0, 1, 0)
-        res0 = tile("res0", [P, 4, E], F32)
-        nc.vector.tensor_tensor(out=res0[:], in0=y0[:], in1=inv0[:].unsqueeze(2).to_broadcast([P, 4, E]), op=ALU.mult)
-        store(res0, 0, 0, 4)
-        quantize_w(5, QT, 2 * QT)
-        values(y1, 1, 1, 1)
-        cap(6, 2)
-        cap(6, 3)
-        exp(5, 2 * QT, 3 * QT)
-        exp(6, 0, QT // 2)
-        exp(6, QT // 2, QT)
-        y2 = ps.tile([P, 4, E], F32, name="y2", tag="y0")
-        values_pass(y2, 0, 1, 3, 0)
-        weigh(5, 2 * QT, 3 * QT)
-        weigh(6, 0, QT // 2)
-        quantize_w(5, 2 * QT, 3 * QT)
-        values(y1, 2, 1, 2)
-        weigh(6, QT // 2, QT)
-        quantize_w(6, 0, QT // 2)
-        quantize_w(6, QT // 2, QT)
-        values_pass(y2, 0, 1, 3, 1)
-        den1 = denominators(y1, 1, 0, 3)
+        den1 = denominators(ys[1], 1, 0, 3)
         inv1 = invert(den1, 1, 0, 3)
-        den2 = denominators(y2, 1, 3, 1)
+        values_pass(y_last, 0, 1, 3, 1)
+        scale_rows_act(ys[1], inv1, 1, 0, 3)
+        den2 = denominators(y_last, 1, 3, 1)
         inv2 = invert(den2, 1, 3, 1)
-        res1 = tile("res1", [P, 3, E], F32)
-        for x in range(3):
-            nc.scalar.activation(out=res1[:, x, :], in_=y1[:, x, :], func=ACT.Copy, scale=inv1[:, x:x + 1])
-        store(res1, 1, 0, 3)
-        res2 = tile("res2", [P, 1, E], F32)
-        nc.vector.tensor_scalar(out=res2[:, 0, :], in0=y2[:, 0, :], scalar1=inv2[:, 0:1], scalar2=None, op0=ALU.mult)
-        store(res2, 1, 3, 1)
+        scale_rows(y_last, inv2, 1, 3, 1)

@@ -43,10 +43,10 @@ def tile_rows_a_exp_kb_cap_sink_kernel(tc, qT, kT, t, v, kb, sink, out):
             return raw
 
         half = PASS // 2
+        t_sb = load("t", t.rearrange("(c p r) o -> p c (r o)", p=P, r=PACK), nc.sync)
         k0a = load("k0a", k_hbm[:, :, 0:half], nc.sync)
         k0b = load("k0b", k_hbm[:, :, half:PASS], nc.sync)
         q0 = load("q0", q_hbm[:, :, 0:QT], nc.sync)
-        t_sb = load("t", t.rearrange("(c p r) o -> p c (r o)", p=P, r=PACK), nc.scalar)
         kb_sb = load("kb", kb.rearrange("(c p r) o -> p c (r o)", p=P, r=PACK), nc.scalar)
         q1 = load("q1", q_hbm[:, :, QT:NQ], nc.sync)
         k1 = load("k1", k_hbm[:, :, PASS:N], nc.sync)
@@ -190,9 +190,11 @@ def tile_rows_a_exp_kb_cap_sink_kernel(tc, qT, kT, t, v, kb, sink, out):
         def store(res, g, a, n):
             nc.sync.dma_start(out=out[g, a * QT:(a + n) * QT, :].rearrange("(x p) e -> p x e", p=P), in_=res[:])
 
-        nc.scalar.activation(out=abs_t[:], in_=t_sb[:], func=ACT.Abs)
-        nc.scalar.activation(out=kb_half[:], in_=kb_sb[:], func=ACT.Copy, scale=1.0 / CAP)
+        flat_t = t_sb[:].rearrange("p c r -> p (c r)")
+        nc.vector.scalar_tensor_tensor(out=abs_t[:].rearrange("p c r -> p (c r)"), in0=flat_t, scalar=-1.0, in1=flat_t,
+                                       op0=ALU.mult, op1=ALU.max)
         nc.scalar.activation(out=log_t[:], in_=abs_t[:], func=ACT.Ln)
+        nc.scalar.activation(out=kb_half[:], in_=kb_sb[:], func=ACT.Copy, scale=1.0 / CAP)
         round_keys(0, k0a, 0)
         round_keys(0, k0b, half // PACK)
         round_queries(0, q0, 0, QT)
@@ -204,6 +206,7 @@ def tile_rows_a_exp_kb_cap_sink_kernel(tc, qT, kT, t, v, kb, sink, out):
         issue_scores()
         nc.vector.tensor_scalar(out=positive[:], in0=t_sb[:], scalar1=0.0, scalar2=2.0, op0=ALU.is_ge, op1=ALU.mult)
         round_queries(1, q1, 0, QT)
+        nc.vector.tensor_scalar(out=sign_t[:], in0=positive[:], scalar1=1.0, scalar2=None, op0=ALU.subtract)
         round_queries(1, q1, QT, 3 * QT)
         quantize(q_codes[1], q_scales[1], q16[1], 0, QT)
         quantize(q_codes[1], q_scales[1], q16[1], QT, 3 * QT)
@@ -231,7 +234,6 @@ def tile_rows_a_exp_kb_cap_sink_kernel(tc, qT, kT, t, v, kb, sink, out):
 
         scalar_group(0)
         weigh(0, 3)
-        nc.vector.tensor_scalar(out=sign_t[:], in0=positive[:], scalar1=1.0, scalar2=None, op0=ALU.subtract)
         round_keys(1, k1, 0)
         quantize(k_codes[1], k_scales[1], k16[1], 0, 2 * P)
         quantize(k_codes[1], k_scales[1], k16[1], 2 * P, 4 * P)
@@ -251,8 +253,9 @@ def tile_rows_a_exp_kb_cap_sink_kernel(tc, qT, kT, t, v, kb, sink, out):
         cap(3, 0)
         weigh(2, 3)
         interleave(2, 0, 2 * QT)
-        interleave(2, 2 * QT, 5 * QT)
+        interleave(2, 2 * QT, 4 * QT)
         quantize_w(2, 0, 2 * QT)
+        interleave(2, 4 * QT, 5 * QT)
         quantize_w(2, 2 * QT, 4 * QT)
         quantize_w(2, 4 * QT, 5 * QT)
         cap(3, 1)
@@ -272,9 +275,12 @@ def tile_rows_a_exp_kb_cap_sink_kernel(tc, qT, kT, t, v, kb, sink, out):
         interleave(3, 0, QT)
         inv = invert(den, 0, 0, 4)
         interleave(3, QT, 3 * QT)
+        den = denominators(ys[1], 1, 0, 1)
         scale_rows(ys[0], inv, 0, 0, 4)
+        inv = invert(den, 1, 0, 1)
         quantize_w(3, 0, QT)
         quantize_w(3, QT, 3 * QT)
+        scale_rows(ys[1], inv, 1, 0, 1)
         for r in range(1, PACK):
             cap(4, r)
             weigh(4, r - 1)
@@ -290,17 +296,21 @@ def tile_rows_a_exp_kb_cap_sink_kernel(tc, qT, kT, t, v, kb, sink, out):
         interleave(4, QT, 2 * QT)
         quantize_w(4, 0, QT)
         quantize_w(4, QT, 2 * QT)
+        y_mid = ps.tile([P, 4, E], F32, name="y_mid", tag="y1")
         for x in range(2):
-            values(ys[1], 1 + x, 1, 1 + x)
+            values(y_mid, x, 1, 1 + x)
         weigh(5, 1)
         weigh(5, 2)
-        weigh(5, 3)
-        interleave(5, 0, QT)
-        quantize_w(5, 0, QT)
-        den1 = denominators(ys[1], 1, 0, 3)
-        inv1 = invert(den1, 1, 0, 3)
+        weigh(5, 3, 0, QT // 2)
+        weigh(5, 3, QT // 2, QT)
+        interleave(5, 0, QT // 2)
+        interleave(5, QT // 2, QT)
+        quantize_w(5, 0, QT // 2)
+        quantize_w(5, QT // 2, QT)
+        den1 = denominators(y_mid, 1, 1, 2)
+        inv1 = invert(den1, 1, 1, 2)
         values_pass(y_last, 0, 1, 3, 1)
-        scale_rows_act(ys[1], inv1, 1, 0, 3)
+        scale_rows_act(y_mid, inv1, 1, 1, 2)
         den2 = denominators(y_last, 1, 3, 1)
         inv2 = invert(den2, 1, 3, 1)
         scale_rows(y_last, inv2, 1, 3, 1)

@@ -20,8 +20,19 @@ ROWS = D // PACK
 PASS = P * PACK
 PASSES = N // PASS
 QT = 128
+TILES = NQ // QT
+BANK = 512
 SCORE_BANKS = 3
 RUN = 4
+
+GROUPS = [
+    (0, [(0, 0, 1), (1, 0, 1)]),
+    (0, [(0, 1, 3)]),
+    (1, [(0, 0, 4), (1, 0, 1)]),
+    (0, [(1, 1, 3)]),
+    (1, [(1, 1, 2)]),
+    (1, [(1, 3, 1)]),
+]
 
 
 def tile_rows_a_exp_kb_cap_sink_kernel(tc, qT, kT, t, v, kb, sink, out):
@@ -34,283 +45,277 @@ def tile_rows_a_exp_kb_cap_sink_kernel(tc, qT, kT, t, v, kb, sink, out):
         def tile(name, shape, dtype):
             return sb.tile(shape, dtype, name=name, tag=name, align_bytes=64)
 
-        q_hbm = qT.rearrange("h (p j) n -> (h p) j n", j=PACK)
-        k_hbm = kT.rearrange("h (p j) n -> (h p) j n", j=PACK)
-
         def load(name, src, queue):
             raw = tile(name, list(src.shape), F32)
             queue.dma_start(out=raw[:], in_=src)
             return raw
 
+        q_hbm = qT.rearrange("h (p j) n -> (h p) j n", j=PACK)
+        k_hbm = kT.rearrange("h (p j) n -> (h p) j n", j=PACK)
         half = PASS // 2
         t_sb = load("t", t.rearrange("(c p r) o -> p c (r o)", p=P, r=PACK), nc.sync)
-        k0a = load("k0a", k_hbm[:, :, 0:half], nc.sync)
-        k0b = load("k0b", k_hbm[:, :, half:PASS], nc.sync)
-        q0 = load("q0", q_hbm[:, :, 0:QT], nc.sync)
+        k_raw = [load("k_raw%d" % x, k_hbm[:, :, x * half:(x + 1) * half], nc.sync) for x in range(2)]
+        q_raw = [load("q_raw0", q_hbm[:, :, 0:QT], nc.sync)]
         kb_sb = load("kb", kb.rearrange("(c p r) o -> p c (r o)", p=P, r=PACK), nc.scalar)
-        q1 = load("q1", q_hbm[:, :, QT:NQ], nc.sync)
-        k1 = load("k1", k_hbm[:, :, PASS:N], nc.sync)
-        v_raw = load("v", v.rearrange("h (c p r) e -> p (h c) (r e)", p=P, r=PACK), nc.sync)
-        sink_sb = tile("sink", [P, H * NQ // QT], F32)
+        q_raw.append(load("q_raw1", q_hbm[:, :, QT:2 * QT], nc.sync))
+        q_raw.append(load("q_raw2", q_hbm[:, :, 2 * QT:NQ], nc.sync))
+        k_raw.extend([load("k_raw%d" % x, k_hbm[:, :, x * half:(x + 1) * half], nc.sync) for x in range(2, 4)])
+        v_raw = load("v_raw", v.rearrange("h (c p r) e -> p (h c) (r e)", p=P, r=PACK), nc.sync)
+        sink_sb = tile("sink", [P, H * TILES], F32)
         with nc.allow_non_contiguous_dma(reason="one sink value a partition and query tile"):
-            nc.sync.dma_start(out=sink_sb[:], in_=sink.rearrange("h (a p) o -> p (h a o)", p=P))
+            nc.sync.dma_start(out=sink_sb[:], in_=sink.rearrange("h (x p) o -> p (h x o)", p=P))
 
-        def quantize(codes, scales, src, a, b):
-            nc.vector.quantize_mx(out=codes[:, a:b].bitcast(FP8X4), scales=scales[:, a:b],
-                                  in_=src[:, PACK * a:PACK * b])
+        def operand(name, columns):
+            return (tile(name + "_bf16", [P, columns * PACK], BF16), tile(name + "_codes", [P, columns], U32),
+                    tile(name + "_scales", [P, columns], U8))
 
-        k16 = [tile("k16_%d" % c, [P, PASS * PACK], BF16) for c in range(PASSES)]
-        k_codes = [tile("kc%d" % c, [P, PASS], U32) for c in range(PASSES)]
-        k_scales = [tile("ks%d" % c, [P, PASS], U8) for c in range(PASSES)]
-        q16 = [tile("q16_0", [P, QT * PACK], BF16), tile("q16_1", [P, (NQ - QT) * PACK], BF16)]
-        q_codes = [tile("qc0", [P, QT], U32), tile("qc1", [P, NQ - QT], U32)]
-        q_scales = [tile("qs0", [P, QT], U8), tile("qs1", [P, NQ - QT], U8)]
-        v16 = tile("v16", [P, H * PASSES * E * PACK], BF16)
-        v_codes = tile("vc", [P, H * PASSES * E], U32)
-        v_scales = tile("vs", [P, H * PASSES * E], U8)
-        kb_half = tile("kbh", [P, PASSES, PACK], F32)
-        positive = tile("positive", [P, PASSES, PACK], F32)
+        def quantize(mx, first, last):
+            values, codes, scales = mx
+            nc.vector.quantize_mx(out=codes[:, first:last].bitcast(FP8X4), scales=scales[:, first:last],
+                                  in_=values[:, PACK * first:PACK * last])
+
+        widths = [sum(count for (g, qt0, count) in parts) * QT for (c, parts) in GROUPS]
+        k_mx = [operand("k%d" % c, PASS) for c in range(PASSES)]
+        q_mx = [operand("q_first", QT), operand("q_rest", NQ - QT)]
+        v_mx = operand("v", H * PASSES * E)
+        w_mx = [operand("w%d" % i, width) for i, width in enumerate(widths)]
+
+        kb_scaled = tile("kb_scaled", [P, PASSES, PACK], F32)
+        twice_positive = tile("twice_positive", [P, PASSES, PACK], F32)
         sign_t = tile("sign_t", [P, PASSES, PACK], F32)
         abs_t = tile("abs_t", [P, PASSES, PACK], F32)
         log_t = tile("log_t", [P, PASSES, PACK], F32)
 
-        def round_keys(c, raw, s0):
-            n = raw.shape[2] // PACK
-            dst = k16[c][:].rearrange("p (r s j) -> p s j r", r=PACK, j=PACK)
-            nc.vector.tensor_copy(out=dst[:, s0:s0 + n], in_=raw[:].rearrange("p j (s r) -> p s j r", r=PACK))
+        def round_keys(x):
+            s0 = (x % 2) * half // PACK
+            dealt = k_mx[x // 2][0][:].rearrange("p (r s j) -> p s j r", r=PACK, j=PACK)
+            nc.vector.tensor_copy(out=dealt[:, s0:s0 + half // PACK],
+                                  in_=k_raw[x][:].rearrange("p j (s r) -> p s j r", r=PACK))
 
-        def round_queries(x, raw, a, b):
-            nc.vector.tensor_copy(out=q16[x][:, PACK * a:PACK * b].rearrange("p (a i j) -> p a j i", i=RUN, j=PACK),
-                                  in_=raw[:, :, a:b].rearrange("p j (a i) -> p a j i", i=RUN))
+        def round_queries(raw, mx, first, last):
+            nc.vector.tensor_copy(
+                out=mx[0][:, PACK * first:PACK * last].rearrange("p (a i j) -> p a j i", i=RUN, j=PACK),
+                in_=raw[:].rearrange("p j (a i) -> p a j i", i=RUN))
 
         def round_values(c):
+            signs = sign_t[:, c, :].unsqueeze(1).unsqueeze(3).to_broadcast([P, E // RUN, PACK, RUN])
             for g in range(H):
                 x = g * PASSES + c
                 nc.vector.tensor_tensor(
-                    out=v16[:, x * PASS:(x + 1) * PASS].rearrange("p (a i r) -> p a r i", i=RUN, r=PACK),
-                    in0=v_raw[:, x, :].rearrange("p (r a i) -> p a r i", r=PACK, i=RUN),
-                    in1=sign_t[:, c, :].unsqueeze(1).unsqueeze(3).to_broadcast([P, E // RUN, PACK, RUN]),
-                    op=ALU.mult)
+                    out=v_mx[0][:, x * PASS:(x + 1) * PASS].rearrange("p (a i r) -> p a r i", i=RUN, r=PACK),
+                    in0=v_raw[:, x, :].rearrange("p (r a i) -> p a r i", r=PACK, i=RUN), in1=signs, op=ALU.mult)
 
-        def q_operand(g, qt):
-            x = min(qt, 1)
-            cols = slice((qt - x) * QT, (qt - x + 1) * QT)
-            rows = slice(ROWS * g, ROWS * (g + 1))
-            return q_codes[x][rows, cols], q_scales[x][rows, cols]
+        capped = [tile("capped%d" % i, [P, PACK, width], F32) for i, width in enumerate(widths)]
+        weights = [tile("weights%d" % i, [P, PACK, width], BF16) for i, width in enumerate(widths)]
+        waiting = [(i, r) for i in range(len(GROUPS)) for r in range(PACK)]
+        quantised_groups = set()
+        score_bank = {}
+        banks_filled = [0] * H
+        banks_read = [0] * H
 
-        groups = [(0, [(0, 0, 1), (1, 0, 1)]), (0, [(0, 1, 3)]), (1, [(0, 0, 4), (1, 0, 1)]), (0, [(1, 1, 3)]), (1, [(1, 1, 2)]), (1, [(1, 3, 1)])]
-        widths = [sum(n for (g, a, n) in parts) * QT for (c, parts) in groups]
-        capped = [tile("th%d" % i, [P, PACK, w], F32) for i, w in enumerate(widths)]
-        rounded = [tile("p%d" % i, [P, PACK, w], BF16) for i, w in enumerate(widths)]
-        w16 = [tile("w16_%d" % i, [P, w * PACK], BF16) for i, w in enumerate(widths)]
-        w_codes = [tile("wc%d" % i, [P, w], U32) for i, w in enumerate(widths)]
-        w_scales = [tile("ws%d" % i, [P, w], U8) for i, w in enumerate(widths)]
-        pending = [(i, r) for i in range(len(groups)) for r in range(PACK)]
-        banks = {}
-        issued = [0, 0]
-        freed = [0, 0]
-        ready = set()
-
-        def issue_scores():
-            while pending and pending[0][0] in ready:
-                i, r = pending[0]
-                c, parts = groups[i]
-                if any(issued[g] - freed[g] == SCORE_BANKS for (g, a, n) in parts):
+        def multiply_scores():
+            while waiting and waiting[0][0] in quantised_groups:
+                i, r = waiting[0]
+                c, parts = GROUPS[i]
+                if any(banks_filled[g] - banks_read[g] == SCORE_BANKS for (g, qt0, count) in parts):
                     return
-                pending.remove((i, r))
-                for (g, a, n) in parts:
-                    tag = "s%d_%d" % (g, issued[g] % SCORE_BANKS)
-                    issued[g] = issued[g] + 1
-                    banks[(i, r, g)] = ps.tile([P, 512], F32, name=tag, tag=tag)
-                cols = slice(r * P, (r + 1) * P)
-                for x in range(4):
-                    for (g, a, n) in [part for part in parts if x < part[2]]:
+                waiting.remove((i, r))
+                for (g, qt0, count) in parts:
+                    tag = "scores%d_%d" % (g, banks_filled[g] % SCORE_BANKS)
+                    banks_filled[g] = banks_filled[g] + 1
+                    score_bank[(i, r, g)] = ps.tile([P, BANK], F32, name=tag, tag=tag)
+                tokens = slice(r * P, (r + 1) * P)
+                for x in range(TILES):
+                    for (g, qt0, count) in [part for part in parts if x < part[2]]:
                         rows = slice(ROWS * g, ROWS * (g + 1))
-                        qc, qs = q_operand(g, a + x)
-                        nc.tensor.matmul_mx(out=banks[(i, r, g)][:, x * QT:(x + 1) * QT],
-                                            lhsT=k_codes[c][rows, cols].bitcast(FP8X4),
-                                            lhsT_scale=k_scales[c][rows, cols], rhs=qc.bitcast(FP8X4), rhs_scale=qs,
-                                            start=True, stop=True)
+                        rest = min(qt0 + x, 1)
+                        queries = slice((qt0 + x - rest) * QT, (qt0 + x - rest + 1) * QT)
+                        nc.tensor.matmul_mx(
+                            out=score_bank[(i, r, g)][:, x * QT:(x + 1) * QT],
+                            lhsT=k_mx[c][1][rows, tokens].bitcast(FP8X4), lhsT_scale=k_mx[c][2][rows, tokens],
+                            rhs=q_mx[rest][1][rows, queries].bitcast(FP8X4), rhs_scale=q_mx[rest][2][rows, queries],
+                            start=True, stop=True)
 
         def cap(i, r):
-            c, parts = groups[i]
+            c, parts = GROUPS[i]
             first = 0
-            for (g, a, n) in parts:
-                nc.scalar.activation(out=capped[i][:, r, first:first + n * QT], in_=banks[(i, r, g)][:, 0:n * QT],
-                                     func=ACT.Tanh, bias=kb_half[:, c, r:r + 1], scale=1.0 / CAP)
-                freed[g] = freed[g] + 1
-                first = first + n * QT
-            issue_scores()
+            for (g, qt0, count) in parts:
+                nc.scalar.activation(out=capped[i][:, r, first:first + count * QT],
+                                     in_=score_bank[(i, r, g)][:, 0:count * QT], func=ACT.Tanh,
+                                     bias=kb_scaled[:, c, r:r + 1], scale=1.0 / CAP)
+                banks_read[g] = banks_read[g] + 1
+                first = first + count * QT
+            multiply_scores()
 
-        def weigh(i, r, a=0, b=None):
-            b = widths[i] if b is None else b
-            nc.scalar.activation(out=rounded[i][:, r, a:b], in_=capped[i][:, r, a:b], func=ACT.Exp, scale=CAP,
-                                 bias=log_t[:, groups[i][0], r:r + 1])
+        def weigh_columns(i, r, first, last):
+            nc.scalar.activation(out=weights[i][:, r, first:last], in_=capped[i][:, r, first:last], func=ACT.Exp,
+                                 scale=CAP, bias=log_t[:, GROUPS[i][0], r:r + 1])
 
-        def interleave(i, a, b):
-            nc.vector.tensor_copy(
-                out=w16[i][:, PACK * a:PACK * b].rearrange("p (a i r) -> p a r i", i=RUN, r=PACK),
-                in_=rounded[i][:, :, a:b].rearrange("p r (a i) -> p a r i", i=RUN))
+        def weigh(i, r):
+            weigh_columns(i, r, 0, widths[i])
 
-        def quantize_w(i, a, b):
-            quantize(w_codes[i], w_scales[i], w16[i], a, b)
-
-        w_place = {}
-        for i, (c, parts) in enumerate(groups):
-            tiles = [(g, a + x) for (g, a, n) in parts for x in range(n)]
-            for x, (g, qt) in enumerate(tiles):
-                w_place[(c, g, qt)] = (i, slice(x * QT, (x + 1) * QT))
-
-        def w_operand(c, g, qt):
-            i, cols = w_place[(c, g, qt)]
-            return w_codes[i][:, cols], w_scales[i][:, cols]
-
-        def values_pass(y, x, g, qt, c):
-            wc, ws = w_operand(c, g, qt)
-            cols = slice((g * PASSES + c) * E, (g * PASSES + c + 1) * E)
-            nc.tensor.matmul_mx(out=y[:, x, :], lhsT=wc.bitcast(FP8X4), lhsT_scale=ws,
-                                rhs=v_codes[:, cols].bitcast(FP8X4), rhs_scale=v_scales[:, cols],
-                                start=(c == 0), stop=(c == PASSES - 1))
-
-        def values(y, x, g, qt):
-            for c in range(PASSES):
-                values_pass(y, x, g, qt, c)
-
-        def denominators(y, g, a, n):
-            den = tile("den%d_%d" % (g, a), [P, n], F32)
-            col = g * (NQ // QT) + a
-            nc.vector.tensor_tensor(out=den[:], in0=y[:, 0:n, E - 1], in1=sink_sb[:, col:col + n], op=ALU.add)
-            return den
-
-        def invert(den, g, a, n):
-            inv = tile("inv%d_%d" % (g, a), [P, n], F32)
-            nc.vector.reciprocal(out=inv[:], in_=den[:])
-            return inv
-
-        def store(res, g, a, n):
-            nc.sync.dma_start(out=out[g, a * QT:(a + n) * QT, :].rearrange("(x p) e -> p x e", p=P), in_=res[:])
-
-        flat_t = t_sb[:].rearrange("p c r -> p (c r)")
-        nc.vector.scalar_tensor_tensor(out=abs_t[:].rearrange("p c r -> p (c r)"), in0=flat_t, scalar=-1.0, in1=flat_t,
-                                       op0=ALU.mult, op1=ALU.max)
-        nc.scalar.activation(out=log_t[:], in_=abs_t[:], func=ACT.Ln)
-        nc.scalar.activation(out=kb_half[:], in_=kb_sb[:], func=ACT.Copy, scale=1.0 / CAP)
-        round_keys(0, k0a, 0)
-        round_keys(0, k0b, half // PACK)
-        round_queries(0, q0, 0, QT)
-        quantize(k_codes[0], k_scales[0], k16[0], 0, P)
-        quantize(q_codes[0], q_scales[0], q16[0], 0, QT)
-        quantize(k_codes[0], k_scales[0], k16[0], P, 2 * P)
-        quantize(k_codes[0], k_scales[0], k16[0], 2 * P, 4 * P)
-        ready.add(0)
-        issue_scores()
-        nc.vector.tensor_scalar(out=positive[:], in0=t_sb[:], scalar1=0.0, scalar2=2.0, op0=ALU.is_ge, op1=ALU.mult)
-        round_queries(1, q1, 0, QT)
-        nc.vector.tensor_scalar(out=sign_t[:], in0=positive[:], scalar1=1.0, scalar2=None, op0=ALU.subtract)
-        round_queries(1, q1, QT, 3 * QT)
-        quantize(q_codes[1], q_scales[1], q16[1], 0, QT)
-        quantize(q_codes[1], q_scales[1], q16[1], QT, 3 * QT)
-        ready.add(1)
-
-        def scale_rows(y, inv, g, a, n):
-            res = tile("res%d_%d" % (g, a), [P, n, E], F32)
-            nc.vector.tensor_tensor(out=res[:], in0=y[:, 0:n, :], in1=inv[:].unsqueeze(2).to_broadcast([P, n, E]),
-                                    op=ALU.mult)
-            store(res, g, a, n)
-
-        def scale_rows_act(y, inv, g, a, n):
-            res = tile("res%d_%d" % (g, a), [P, n, E], F32)
-            for x in range(n):
-                nc.scalar.activation(out=res[:, x, :], in_=y[:, x, :], func=ACT.Copy, scale=inv[:, x:x + 1])
-            store(res, g, a, n)
-
-        def scalar_group(i):
-            for r in range(PACK):
+        def cap_and_weigh(i, places):
+            for r in places:
                 cap(i, r)
                 if r > 0:
                     weigh(i, r - 1)
-                elif i > 1:
+                else:
                     weigh(i - 1, PACK - 1)
 
-        scalar_group(0)
-        weigh(0, 3)
-        round_keys(1, k1, 0)
-        quantize(k_codes[1], k_scales[1], k16[1], 0, 2 * P)
-        quantize(k_codes[1], k_scales[1], k16[1], 2 * P, 4 * P)
-        for i in (2, 3, 4, 5):
-            ready.add(i)
-        scalar_group(1)
+        def interleave(i, first, last):
+            nc.vector.tensor_copy(
+                out=w_mx[i][0][:, PACK * first:PACK * last].rearrange("p (a i r) -> p a r i", i=RUN, r=PACK),
+                in_=weights[i][:, :, first:last].rearrange("p r (a i) -> p a r i", i=RUN))
+
+        w_columns = {}
+        for i, (c, parts) in enumerate(GROUPS):
+            members = [(g, qt0 + x) for (g, qt0, count) in parts for x in range(count)]
+            for x, (g, qt) in enumerate(members):
+                w_columns[(c, g, qt)] = (i, slice(x * QT, (x + 1) * QT))
+
+        def y_bank(name, tag):
+            return ps.tile([P, TILES, E], F32, name=name, tag=tag)
+
+        def multiply_values_pass(y, x, g, qt, c):
+            i, queries = w_columns[(c, g, qt)]
+            features = slice((g * PASSES + c) * E, (g * PASSES + c + 1) * E)
+            nc.tensor.matmul_mx(out=y[:, x, :], lhsT=w_mx[i][1][:, queries].bitcast(FP8X4),
+                                lhsT_scale=w_mx[i][2][:, queries], rhs=v_mx[1][:, features].bitcast(FP8X4),
+                                rhs_scale=v_mx[2][:, features], start=(c == 0), stop=(c == PASSES - 1))
+
+        def multiply_values(y, x, g, qt):
+            for c in range(PASSES):
+                multiply_values_pass(y, x, g, qt, c)
+
+        def denominators(y, g, qt0, count):
+            den = tile("den%d_%d" % (g, qt0), [P, count], F32)
+            column = g * TILES + qt0
+            nc.vector.tensor_tensor(out=den[:], in0=y[:, 0:count, E - 1], in1=sink_sb[:, column:column + count],
+                                    op=ALU.add)
+            return den
+
+        def invert(den, g, qt0, count):
+            inv = tile("inv%d_%d" % (g, qt0), [P, count], F32)
+            nc.vector.reciprocal(out=inv[:], in_=den[:])
+            return inv
+
+        def store(res, g, qt0, count):
+            rows = out[g, qt0 * QT:(qt0 + count) * QT, :]
+            nc.sync.dma_start(out=rows.rearrange("(x p) e -> p x e", p=P), in_=res[:])
+
+        def divide_on_vector(y, inv, g, qt0, count):
+            res = tile("res%d_%d" % (g, qt0), [P, count, E], F32)
+            nc.vector.tensor_tensor(out=res[:], in0=y[:, 0:count, :],
+                                    in1=inv[:].unsqueeze(2).to_broadcast([P, count, E]), op=ALU.mult)
+            store(res, g, qt0, count)
+
+        def divide_on_scalar(y, inv, g, qt0, count):
+            res = tile("res%d_%d" % (g, qt0), [P, count, E], F32)
+            for x in range(count):
+                nc.scalar.activation(out=res[:, x, :], in_=y[:, x, :], func=ACT.Copy, scale=inv[:, x:x + 1])
+            store(res, g, qt0, count)
+
+        t_flat = t_sb[:].rearrange("p c r -> p (c r)")
+        nc.vector.scalar_tensor_tensor(out=abs_t[:].rearrange("p c r -> p (c r)"), in0=t_flat, scalar=-1.0,
+                                       in1=t_flat, op0=ALU.mult, op1=ALU.max)
+        nc.scalar.activation(out=log_t[:], in_=abs_t[:], func=ACT.Ln)
+        round_keys(0)
+        nc.vector.tensor_scalar(out=kb_scaled[:], in0=kb_sb[:], scalar1=1.0 / CAP, scalar2=None, op0=ALU.mult)
+        round_keys(1)
+        round_queries(q_raw[0], q_mx[0], 0, QT)
+        quantize(k_mx[0], 0, P)
+        quantize(q_mx[0], 0, QT)
+        quantize(k_mx[0], P, 2 * P)
+        quantize(k_mx[0], 2 * P, 4 * P)
+        quantised_groups.add(0)
+        multiply_scores()
+
+        nc.vector.tensor_scalar(out=twice_positive[:], in0=t_sb[:], scalar1=0.0, scalar2=2.0, op0=ALU.is_ge,
+                                op1=ALU.mult)
+        round_queries(q_raw[1], q_mx[1], 0, QT)
+        nc.vector.tensor_scalar(out=sign_t[:], in0=twice_positive[:], scalar1=1.0, scalar2=None, op0=ALU.subtract)
+        round_queries(q_raw[2], q_mx[1], QT, 3 * QT)
+        quantize(q_mx[1], 0, QT)
+        quantize(q_mx[1], QT, 3 * QT)
+        quantised_groups.add(1)
+        cap(0, 0)
+        cap_and_weigh(0, range(1, PACK))
+        weigh(0, PACK - 1)
+        round_keys(2)
+        round_keys(3)
+        quantize(k_mx[1], 0, 2 * P)
+        quantize(k_mx[1], 2 * P, 4 * P)
+        for i in range(2, len(GROUPS)):
+            quantised_groups.add(i)
+
+        cap(1, 0)
+        cap_and_weigh(1, range(1, PACK))
         interleave(0, 0, 2 * QT)
         round_values(0)
-        quantize_w(0, 0, 2 * QT)
-        scalar_group(2)
+        quantize(w_mx[0], 0, 2 * QT)
+        cap_and_weigh(2, range(PACK))
         interleave(1, 0, 3 * QT)
         round_values(1)
-        quantize_w(1, 0, QT)
-        quantize_w(1, QT, 3 * QT)
-        quantize(v_codes, v_scales, v16, 0, H * PASSES * E)
-        ys = [ps.tile([P, 4, E], F32, name="y%d" % x, tag="y%d" % x) for x in range(2)]
-        cap(3, 0)
-        weigh(2, 3)
+        quantize(w_mx[1], 0, QT)
+        quantize(w_mx[1], QT, 3 * QT)
+        quantize(v_mx, 0, H * PASSES * E)
+
+        y_head0 = y_bank("y_head0", "y_a")
+        y_first = y_bank("y_first", "y_b")
+        cap_and_weigh(3, [0])
         interleave(2, 0, 2 * QT)
         interleave(2, 2 * QT, 4 * QT)
-        quantize_w(2, 0, 2 * QT)
+        quantize(w_mx[2], 0, 2 * QT)
         interleave(2, 4 * QT, 5 * QT)
-        quantize_w(2, 2 * QT, 4 * QT)
-        quantize_w(2, 4 * QT, 5 * QT)
-        cap(3, 1)
-        weigh(3, 0)
-        cap(3, 2)
-        values(ys[0], 0, 0, 0)
-        values(ys[0], 1, 0, 1)
-        weigh(3, 1)
-        cap(3, 3)
-        values(ys[0], 2, 0, 2)
-        values(ys[0], 3, 0, 3)
-        weigh(3, 2)
-        cap(4, 0)
-        values(ys[1], 0, 1, 0)
-        weigh(3, 3)
-        den = denominators(ys[0], 0, 0, 4)
+        quantize(w_mx[2], 2 * QT, 4 * QT)
+        quantize(w_mx[2], 4 * QT, 5 * QT)
+        cap_and_weigh(3, [1, 2])
+        multiply_values(y_head0, 0, 0, 0)
+        multiply_values(y_head0, 1, 0, 1)
+        cap_and_weigh(3, [3])
+        multiply_values(y_head0, 2, 0, 2)
+        multiply_values(y_head0, 3, 0, 3)
+
+        cap_and_weigh(4, [0])
+        multiply_values(y_first, 0, 1, 0)
         interleave(3, 0, QT)
-        inv = invert(den, 0, 0, 4)
         interleave(3, QT, 3 * QT)
-        den = denominators(ys[1], 1, 0, 1)
-        scale_rows(ys[0], inv, 0, 0, 4)
-        inv = invert(den, 1, 0, 1)
-        quantize_w(3, 0, QT)
-        quantize_w(3, QT, 3 * QT)
-        scale_rows(ys[1], inv, 1, 0, 1)
-        for r in range(1, PACK):
-            cap(4, r)
-            weigh(4, r - 1)
-        cap(5, 0)
-        weigh(4, 3)
+        den_head0 = denominators(y_head0, 0, 0, TILES)
+        den_first = denominators(y_first, 1, 0, 1)
+        quantize(w_mx[3], 0, QT)
+        inv_head0 = invert(den_head0, 0, 0, TILES)
+        inv_first = invert(den_first, 1, 0, 1)
+        quantize(w_mx[3], QT, 3 * QT)
+        divide_on_vector(y_first, inv_first, 1, 0, 1)
+        cap_and_weigh(4, range(1, PACK))
+
+        cap_and_weigh(5, [0])
         cap(5, 1)
         cap(5, 2)
         weigh(5, 0)
         cap(5, 3)
-        y_last = ps.tile([P, 4, E], F32, name="y_last", tag="y0")
-        values_pass(y_last, 0, 1, 3, 0)
         interleave(4, 0, QT)
         interleave(4, QT, 2 * QT)
-        quantize_w(4, 0, QT)
-        quantize_w(4, QT, 2 * QT)
-        y_mid = ps.tile([P, 4, E], F32, name="y_mid", tag="y1")
-        for x in range(2):
-            values(y_mid, x, 1, 1 + x)
+        quantize(w_mx[4], 0, QT)
+        quantize(w_mx[4], QT, 2 * QT)
+        y_middle = y_bank("y_middle", "y_b")
+        multiply_values(y_middle, 0, 1, 1)
+        multiply_values(y_middle, 1, 1, 2)
         weigh(5, 1)
         weigh(5, 2)
-        weigh(5, 3, 0, QT // 2)
-        weigh(5, 3, QT // 2, QT)
-        interleave(5, 0, QT // 2)
-        interleave(5, QT // 2, QT)
-        quantize_w(5, 0, QT // 2)
-        quantize_w(5, QT // 2, QT)
-        den1 = denominators(y_mid, 1, 1, 2)
-        inv1 = invert(den1, 1, 1, 2)
-        values_pass(y_last, 0, 1, 3, 1)
-        scale_rows_act(y_mid, inv1, 1, 1, 2)
-        den2 = denominators(y_last, 1, 3, 1)
-        inv2 = invert(den2, 1, 3, 1)
-        scale_rows(y_last, inv2, 1, 3, 1)
+
+        halves = [(0, QT // 2), (QT // 2, QT)]
+        for (first, last) in halves:
+            weigh_columns(5, PACK - 1, first, last)
+        divide_on_scalar(y_head0, inv_head0, 0, 0, TILES)
+        y_last = y_bank("y_last", "y_a")
+        multiply_values_pass(y_last, 0, 1, 3, 0)
+        for (first, last) in halves:
+            interleave(5, first, last)
+        for (first, last) in halves:
+            quantize(w_mx[5], first, last)
+        inv_middle = invert(denominators(y_middle, 1, 1, 2), 1, 1, 2)
+        multiply_values_pass(y_last, 0, 1, 3, 1)
+        divide_on_scalar(y_middle, inv_middle, 1, 1, 2)
+        inv_last = invert(denominators(y_last, 1, 3, 1), 1, 3, 1)
+        divide_on_vector(y_last, inv_last, 1, 3, 1)

from contextlib import ExitStack

import concourse.mybir as mybir

H, D, NQ, N, E = 2, 256, 512, 1024, 128
CAP = 2.0
FLOPS = 2 * H * NQ * N * (D + E)

F32 = mybir.dt.float32
BF16 = mybir.dt.bfloat16
U32 = mybir.dt.uint32
U8 = mybir.dt.uint8
FP8X4 = mybir.dt.float8_e4m3fn_x4
ACT = mybir.ActivationFunctionType
ALU = mybir.AluOpType

P = 128
PACK = 4
ROWS = D // PACK
PASS = P * PACK
PASSES = N // PASS
QT = 128
TILES = NQ // QT
BANK = 512
SCORE_BANKS = 3
RUN = 4

GROUPS = [
    (0, [(0, 0, 1), (1, 0, 1)]),
    (0, [(0, 1, 3)]),
    (1, [(0, 0, 4), (1, 0, 1)]),
    (0, [(1, 1, 3)]),
    (1, [(1, 1, 2)]),
    (1, [(1, 3, 1)]),
]


def tile_rows_a_exp_kb_cap_sink_kernel(tc, qT, kT, t, v, kb, sink, out):
    nc = tc.nc
    with ExitStack() as ctx:
        sb = ctx.enter_context(tc.tile_pool(name="sb", bufs=1))
        ps = ctx.enter_context(tc.psum_pool(name="ps", bufs=1))
        ctx.enter_context(tc.manual_schedule())

        def tile(name, shape, dtype):
            return sb.tile(shape, dtype, name=name, tag=name, align_bytes=64)

        def load(name, src, queue):
            raw = tile(name, list(src.shape), F32)
            queue.dma_start(out=raw[:], in_=src)
            return raw

        q_hbm = qT.rearrange("h (p j) n -> (h p) j n", j=PACK)
        k_hbm = kT.rearrange("h (p j) n -> (h p) j n", j=PACK)
        half = PASS // 2
        t_sb = load("t", t.rearrange("(c p r) o -> p c (r o)", p=P, r=PACK), nc.sync)
        k_raw = [load("k_raw%d" % x, k_hbm[:, :, x * half:(x + 1) * half], nc.sync) for x in range(2)]
        q_raw = [load("q_raw0", q_hbm[:, :, 0:QT], nc.sync)]
        kb_sb = load("kb", kb.rearrange("(c p r) o -> p c (r o)", p=P, r=PACK), nc.scalar)
        q_raw.append(load("q_raw1", q_hbm[:, :, QT:2 * QT], nc.sync))
        q_raw.append(load("q_raw2", q_hbm[:, :, 2 * QT:NQ], nc.sync))
        k_raw.extend([load("k_raw%d" % x, k_hbm[:, :, x * half:(x + 1) * half], nc.sync) for x in range(2, 4)])
        v_raw = load("v_raw", v.rearrange("h (c p r) e -> p (h c) (r e)", p=P, r=PACK), nc.sync)
        sink_sb = tile("sink", [P, H * TILES], F32)
        with nc.allow_non_contiguous_dma(reason="one sink value a partition and query tile"):
            nc.sync.dma_start(out=sink_sb[:], in_=sink.rearrange("h (x p) o -> p (h x o)", p=P))

        def operand(name, columns):
            return (tile(name + "_bf16", [P, columns * PACK], BF16), tile(name + "_codes", [P, columns], U32),
                    tile(name + "_scales", [P, columns], U8))

        def quantize(mx, first, last):
            values, codes, scales = mx
            nc.vector.quantize_mx(out=codes[:, first:last].bitcast(FP8X4), scales=scales[:, first:last],
                                  in_=values[:, PACK * first:PACK * last])

        widths = [sum(count for (g, qt0, count) in parts) * QT for (c, parts) in GROUPS]
        k_mx = [operand("k%d" % c, PASS) for c in range(PASSES)]
        q_mx = [operand("q_first", QT), operand("q_rest", NQ - QT)]
        v_mx = operand("v", H * PASSES * E)
        w_mx = [operand("w%d" % i, width) for i, width in enumerate(widths)]

        kb_scaled = tile("kb_scaled", [P, PASSES, PACK], F32)
        twice_positive = tile("twice_positive", [P, PASSES, PACK], F32)
        sign_t = tile("sign_t", [P, PASSES, PACK], F32)
        abs_t = tile("abs_t", [P, PASSES, PACK], F32)
        log_t = tile("log_t", [P, PASSES, PACK], F32)

        def round_keys(x):
            s0 = (x % 2) * half // PACK
            dealt = k_mx[x // 2][0][:].rearrange("p (r s j) -> p s j r", r=PACK, j=PACK)
            nc.vector.tensor_copy(out=dealt[:, s0:s0 + half // PACK],
                                  in_=k_raw[x][:].rearrange("p j (s r) -> p s j r", r=PACK))

        def round_queries(raw, mx, first, last):
            nc.vector.tensor_copy(
                out=mx[0][:, PACK * first:PACK * last].rearrange("p (a i j) -> p a j i", i=RUN, j=PACK),
                in_=raw[:].rearrange("p j (a i) -> p a j i", i=RUN))

        def round_values(c):
            signs = sign_t[:, c, :].unsqueeze(1).unsqueeze(3).to_broadcast([P, E // RUN, PACK, RUN])
            for g in range(H):
                x = g * PASSES + c
                nc.vector.tensor_tensor(
                    out=v_mx[0][:, x * PASS:(x + 1) * PASS].rearrange("p (a i r) -> p a r i", i=RUN, r=PACK),
                    in0=v_raw[:, x, :].rearrange("p (r a i) -> p a r i", r=PACK, i=RUN), in1=signs, op=ALU.mult)

        capped = [tile("capped%d" % i, [P, PACK, width], F32) for i, width in enumerate(widths)]
        weights = [tile("weights%d" % i, [P, PACK, width], BF16) for i, width in enumerate(widths)]
        waiting = [(i, r) for i in range(len(GROUPS)) for r in range(PACK)]
        quantised_groups = set()
        score_bank = {}
        banks_filled = [0] * H
        banks_read = [0] * H

        def multiply_scores():
            while waiting and waiting[0][0] in quantised_groups:
                i, r = waiting[0]
                c, parts = GROUPS[i]
                if any(banks_filled[g] - banks_read[g] == SCORE_BANKS for (g, qt0, count) in parts):
                    return
                waiting.remove((i, r))
                for (g, qt0, count) in parts:
                    tag = "scores%d_%d" % (g, banks_filled[g] % SCORE_BANKS)
                    banks_filled[g] = banks_filled[g] + 1
                    score_bank[(i, r, g)] = ps.tile([P, BANK], F32, name=tag, tag=tag)
                tokens = slice(r * P, (r + 1) * P)
                for x in range(TILES):
                    for (g, qt0, count) in [part for part in parts if x < part[2]]:
                        rows = slice(ROWS * g, ROWS * (g + 1))
                        rest = min(qt0 + x, 1)
                        queries = slice((qt0 + x - rest) * QT, (qt0 + x - rest + 1) * QT)
                        nc.tensor.matmul_mx(
                            out=score_bank[(i, r, g)][:, x * QT:(x + 1) * QT],
                            lhsT=k_mx[c][1][rows, tokens].bitcast(FP8X4), lhsT_scale=k_mx[c][2][rows, tokens],
                            rhs=q_mx[rest][1][rows, queries].bitcast(FP8X4), rhs_scale=q_mx[rest][2][rows, queries],
                            start=True, stop=True)

        def cap(i, r):
            c, parts = GROUPS[i]
            first = 0
            for (g, qt0, count) in parts:
                nc.scalar.activation(out=capped[i][:, r, first:first + count * QT],
                                     in_=score_bank[(i, r, g)][:, 0:count * QT], func=ACT.Tanh,
                                     bias=kb_scaled[:, c, r:r + 1], scale=1.0 / CAP)
                banks_read[g] = banks_read[g] + 1
                first = first + count * QT
            multiply_scores()

        def weigh_columns(i, r, first, last):
            nc.scalar.activation(out=weights[i][:, r, first:last], in_=capped[i][:, r, first:last], func=ACT.Exp,
                                 scale=CAP, bias=log_t[:, GROUPS[i][0], r:r + 1])

        def weigh(i, r):
            weigh_columns(i, r, 0, widths[i])

        def cap_and_weigh(i, places):
            for r in places:
                cap(i, r)
                if r > 0:
                    weigh(i, r - 1)
                else:
                    weigh(i - 1, PACK - 1)

        def interleave(i, first, last):
            nc.vector.tensor_copy(
                out=w_mx[i][0][:, PACK * first:PACK * last].rearrange("p (a i r) -> p a r i", i=RUN, r=PACK),
                in_=weights[i][:, :, first:last].rearrange("p r (a i) -> p a r i", i=RUN))

        w_columns = {}
        for i, (c, parts) in enumerate(GROUPS):
            members = [(g, qt0 + x) for (g, qt0, count) in parts for x in range(count)]
            for x, (g, qt) in enumerate(members):
                w_columns[(c, g, qt)] = (i, slice(x * QT, (x + 1) * QT))

        def y_bank(name, tag):
            return ps.tile([P, TILES, E], F32, name=name, tag=tag)

        def multiply_values_pass(y, x, g, qt, c):
            i, queries = w_columns[(c, g, qt)]
            features = slice((g * PASSES + c) * E, (g * PASSES + c + 1) * E)
            nc.tensor.matmul_mx(out=y[:, x, :], lhsT=w_mx[i][1][:, queries].bitcast(FP8X4),
                                lhsT_scale=w_mx[i][2][:, queries], rhs=v_mx[1][:, features].bitcast(FP8X4),
                                rhs_scale=v_mx[2][:, features], start=(c == 0), stop=(c == PASSES - 1))

        def multiply_values(y, x, g, qt):
            for c in range(PASSES):
                multiply_values_pass(y, x, g, qt, c)

        def denominators(y, g, qt0, count):
            den = tile("den%d_%d" % (g, qt0), [P, count], F32)
            column = g * TILES + qt0
            nc.vector.tensor_tensor(out=den[:], in0=y[:, 0:count, E - 1], in1=sink_sb[:, column:column + count],
                                    op=ALU.add)
            return den

        def invert(den, g, qt0, count):
            inv = tile("inv%d_%d" % (g, qt0), [P, count], F32)
            nc.vector.reciprocal(out=inv[:], in_=den[:])
            return inv

        def store(res, g, qt0, count):
            rows = out[g, qt0 * QT:(qt0 + count) * QT, :]
            nc.sync.dma_start(out=rows.rearrange("(x p) e -> p x e", p=P), in_=res[:])

        def divide_on_vector(y, inv, g, qt0, count):
            res = tile("res%d_%d" % (g, qt0), [P, count, E], F32)
            nc.vector.tensor_tensor(out=res[:], in0=y[:, 0:count, :],
                                    in1=inv[:].unsqueeze(2).to_broadcast([P, count, E]), op=ALU.mult)
            store(res, g, qt0, count)

        def divide_on_scalar(y, inv, g, qt0, count):
            res = tile("res%d_%d" % (g, qt0), [P, count, E], F32)
            for x in range(count):
                nc.scalar.activation(out=res[:, x, :], in_=y[:, x, :], func=ACT.Copy, scale=inv[:, x:x + 1])
            store(res, g, qt0, count)

        t_flat = t_sb[:].rearrange("p c r -> p (c r)")
        nc.vector.scalar_tensor_tensor(out=abs_t[:].rearrange("p c r -> p (c r)"), in0=t_flat, scalar=-1.0,
                                       in1=t_flat, op0=ALU.mult, op1=ALU.max)
        nc.scalar.activation(out=log_t[:], in_=abs_t[:], func=ACT.Ln)
        round_keys(0)
        nc.vector.tensor_scalar(out=kb_scaled[:], in0=kb_sb[:], scalar1=1.0 / CAP, scalar2=None, op0=ALU.mult)
        round_keys(1)
        round_queries(q_raw[0], q_mx[0], 0, QT)
        quantize(k_mx[0], 0, P)
        quantize(q_mx[0], 0, QT)
        quantize(k_mx[0], P, 2 * P)
        quantize(k_mx[0], 2 * P, 4 * P)
        quantised_groups.add(0)
        multiply_scores()

        nc.vector.tensor_scalar(out=twice_positive[:], in0=t_sb[:], scalar1=0.0, scalar2=2.0, op0=ALU.is_ge,
                                op1=ALU.mult)
        round_queries(q_raw[1], q_mx[1], 0, QT)
        nc.vector.tensor_scalar(out=sign_t[:], in0=twice_positive[:], scalar1=1.0, scalar2=None, op0=ALU.subtract)
        round_queries(q_raw[2], q_mx[1], QT, 3 * QT)
        quantize(q_mx[1], 0, QT)
        quantize(q_mx[1], QT, 3 * QT)
        quantised_groups.add(1)
        cap(0, 0)
        cap_and_weigh(0, range(1, PACK))
        weigh(0, PACK - 1)
        round_keys(2)
        round_keys(3)
        quantize(k_mx[1], 0, 2 * P)
        quantize(k_mx[1], 2 * P, 4 * P)
        for i in range(2, len(GROUPS)):
            quantised_groups.add(i)

        cap(1, 0)
        cap_and_weigh(1, range(1, PACK))
        interleave(0, 0, 2 * QT)
        round_values(0)
        quantize(w_mx[0], 0, 2 * QT)
        cap_and_weigh(2, range(PACK))
        interleave(1, 0, 3 * QT)
        round_values(1)
        quantize(w_mx[1], 0, QT)
        quantize(w_mx[1], QT, 3 * QT)
        quantize(v_mx, 0, H * PASSES * E)

        y_head0 = y_bank("y_head0", "y_a")
        y_first = y_bank("y_first", "y_b")
        cap_and_weigh(3, [0])
        interleave(2, 0, 2 * QT)
        interleave(2, 2 * QT, 4 * QT)
        quantize(w_mx[2], 0, 2 * QT)
        interleave(2, 4 * QT, 5 * QT)
        quantize(w_mx[2], 2 * QT, 4 * QT)
        quantize(w_mx[2], 4 * QT, 5 * QT)
        cap_and_weigh(3, [1, 2])
        multiply_values(y_head0, 0, 0, 0)
        multiply_values(y_head0, 1, 0, 1)
        cap_and_weigh(3, [3])
        multiply_values(y_head0, 2, 0, 2)
        multiply_values(y_head0, 3, 0, 3)

        cap_and_weigh(4, [0])
        multiply_values(y_first, 0, 1, 0)
        interleave(3, 0, QT)
        interleave(3, QT, 3 * QT)
        den_head0 = denominators(y_head0, 0, 0, TILES)
        den_first = denominators(y_first, 1, 0, 1)
        quantize(w_mx[3], 0, QT)
        inv_head0 = invert(den_head0, 0, 0, TILES)
        inv_first = invert(den_first, 1, 0, 1)
        quantize(w_mx[3], QT, 3 * QT)
        divide_on_vector(y_first, inv_first, 1, 0, 1)
        cap_and_weigh(4, range(1, PACK))

        cap_and_weigh(5, [0])
        cap(5, 1)
        cap(5, 2)
        weigh(5, 0)
        cap(5, 3)
        interleave(4, 0, QT)
        interleave(4, QT, 2 * QT)
        quantize(w_mx[4], 0, QT)
        quantize(w_mx[4], QT, 2 * QT)
        y_middle = y_bank("y_middle", "y_b")
        multiply_values(y_middle, 0, 1, 1)
        multiply_values(y_middle, 1, 1, 2)
        weigh(5, 1)
        weigh(5, 2)

        halves = [(0, QT // 2), (QT // 2, QT)]
        for (first, last) in halves:
            weigh_columns(5, PACK - 1, first, last)
        divide_on_scalar(y_head0, inv_head0, 0, 0, TILES)
        y_last = y_bank("y_last", "y_a")
        multiply_values_pass(y_last, 0, 1, 3, 0)
        for (first, last) in halves:
            interleave(5, first, last)
        for (first, last) in halves:
            quantize(w_mx[5], first, last)
        inv_middle = invert(denominators(y_middle, 1, 1, 2), 1, 1, 2)
        multiply_values_pass(y_last, 0, 1, 3, 1)
        divide_on_scalar(y_middle, inv_middle, 1, 1, 2)
        inv_last = invert(denominators(y_last, 1, 3, 1), 1, 3, 1)
        divide_on_vector(y_last, inv_last, 1, 3, 1)
